import numpy as np
import ml_dtypes


def mxq(x, axis, fmt="e4m3"):
    dtype, down = {"e4m3": (ml_dtypes.float8_e4m3fn, 7), "e5m2": (ml_dtypes.float8_e5m2, 14)}[fmt]
    v = np.moveaxis(np.asarray(x, np.float32).astype(ml_dtypes.bfloat16).astype(np.float64), axis, -1)
    blocks = v.reshape(v.shape[:-1] + (-1, 32))
    amax = np.abs(blocks).max(-1, keepdims=True)
    byte = np.maximum(np.where(amax > 0, np.frexp(amax)[1] - 1 + 127, 0) - down, 1)
    scale = np.exp2(byte - 127.0)
    codes = (blocks / scale).astype(np.float32).astype(dtype).astype(np.float64)
    return np.moveaxis((codes * scale).reshape(v.shape), -1, axis)


WIDE = False


def mx_kscale(k):
    if not WIDE:
        return np.ones(k)
    levels = np.array([30, -30])
    if k % 512:
        return np.exp2(np.random.permutation(np.resize(levels, k // 32))).repeat(32)
    a = np.empty((k // 512, 16))
    for p in range(k // 512):
        a[p, :8] = np.random.permutation(np.resize(levels, 8))
        for g in range(8):
            far = levels[np.abs(levels - a[p, g]) >= 10]
            a[p, g + 8] = far[np.random.randint(len(far))]
    return np.exp2(a.ravel()).repeat(32)


def f64(x):
    return np.asarray(x).astype(np.float64)


def striped(idx):
    return np.tile(np.asarray(idx).reshape(-1, 16).T, (8, 1)).astype(np.uint16)


def unstriped(offs):
    return offs[:16].T.reshape(-1).astype(np.int64)


E2M1 = np.array([0.0, 0.5, 1.0, 1.5, 2.0, 3.0, 4.0, 6.0, -0.0, -0.5, -1.0, -1.5, -2.0, -3.0, -4.0, -6.0])


def pack_weight(w, fmt):
    k, n = w.shape
    w = f64(np.asarray(w, np.float32).astype(ml_dtypes.bfloat16)).reshape(k // 32, 32, n)
    amax = np.abs(w).max(1)
    if fmt in ("e4m3", "e5m2"):
        byte = np.frexp(amax)[1] - 1 + 127 - (7 if fmt == "e4m3" else 14)
    else:
        mant, ex = np.frexp(amax / 6.0)
        byte = np.where(mant > 0.5, ex, ex - 1) + 127
    byte = np.clip(np.where(amax > 0, byte, 1), 1, 254)
    scaled = (w * np.exp2(127.0 - byte)[:, None, :]).reshape(k, n).astype(np.float32)
    by_word = np.ascontiguousarray(scaled.reshape(k // 512, 128, 4, n).transpose(0, 1, 3, 2))
    if fmt in ("e4m3", "e5m2"):
        words = by_word.astype(ml_dtypes.float8_e4m3fn if fmt == "e4m3" else ml_dtypes.float8_e5m2).view(np.uint8)
    else:
        c = by_word.astype(ml_dtypes.float4_e2m1fn).view(np.uint8) & 0xF
        words = (c[..., 0::2] | (c[..., 1::2] << 4)).reshape(k // 512, 128, 2 * n)
    return np.ascontiguousarray(words), np.ascontiguousarray(byte.astype(np.uint8).reshape(k // 512, 16, n))


def unpack_weight(words, scales, fmt):
    g, _, n = scales.shape
    words = np.ascontiguousarray(words).reshape(g, 128, n, -1)
    if fmt in ("e4m3", "e5m2"):
        vals = words.view(ml_dtypes.float8_e4m3fn if fmt == "e4m3" else ml_dtypes.float8_e5m2).astype(np.float64)
    else:
        nib = np.empty((g, 128, n, 4), np.uint8)
        nib[..., 0::2] = words & 0xF
        nib[..., 1::2] = words >> 4
        vals = E2M1[nib]
    vals = vals * np.repeat(np.exp2(scales.astype(np.float64) - 127.0), 8, axis=1)[..., None]
    return vals.transpose(0, 1, 3, 2).reshape(g * 512, n)


K, T, J, N = 1024, 1024, 256, 256


def setup_inputs():
    n = np.random.standard_normal
    idx = np.random.permutation(T)[:J]
    idx2 = np.random.permutation(T)[:J]
    fk = mx_kscale(K)
    xtp = pack_weight(n((K, T)) * np.random.uniform(0.4, 1.6, (1, T)) / fk[:, None], "e5m2")
    wap = pack_weight(n((K, N)) * 1 / np.sqrt(K) * fk[:, None], "e5m2")
    return {
        "xt_words": xtp[0],
        "xt_scales": xtp[1],
        "wa_words": wap[0],
        "wa_scales": wap[1],
        "wb": (n((K, N)) * 1 / np.sqrt(K) * fk[:, None]).astype(np.float32),
        "bi": (np.random.uniform(-0.6, 0.6, (1, N))).astype(np.float32),
        "offs": striped(idx),
        "offs2": striped(idx2),
    }


def reference(xt_words, xt_scales, wa_words, wa_scales, wb, bi, offs, offs2):
    idx = unstriped(offs)
    idx2 = unstriped(offs2)
    xtu = unpack_weight(xt_words, xt_scales, "e5m2")
    wau = unpack_weight(wa_words, wa_scales, "e5m2")
    xtidxg = xtu[:, idx]
    a = xtidxg.T @ wau
    xtidx2g = xtu[:, idx2]
    wbq = mxq(f64(wb), 0, "e4m3")
    b0 = xtidx2g.T @ wbq
    b2 = b0 + f64(bi)
    pa = np.max(np.abs(a), axis=1, keepdims=True)
    pb = np.max(np.abs(b2), axis=1, keepdims=True)
    y = 0.3 * (a * pb - b2 * pa)
    return y

@@ -1,0 +1,170 @@
+from contextlib import ExitStack
+
+import concourse.mybir as mybir
+from concourse.masks import make_identity
+
+K, T, J, N = 1024, 1024, 256, 256
+FLOPS = 2 * 2 * J * K * N
+
+F32 = mybir.dt.float32
+BF16 = mybir.dt.bfloat16
+I32 = mybir.dt.int32
+U32 = mybir.dt.uint32
+U16 = mybir.dt.uint16
+U8 = mybir.dt.uint8
+E4M3 = mybir.dt.float8_e4m3fn_x4
+E5M2 = mybir.dt.float8_e5m2_x4
+ALU = mybir.AluOpType
+COPY = mybir.ActivationFunctionType.Copy
+AXIS_X = mybir.AxisListType.X
+
+P = 128
+PACK = 4
+PASSES = K // (P * PACK)
+TILES = J // P
+GAIN = 0.3
+
+
+def tile_list_rows_twotokens_crosspeaks_kernel(tc, xt_words, xt_scales, wa_words, wa_scales, wb, bi, offs, offs2, out):
+    nc = tc.nc
+    with ExitStack() as ctx:
+        keep = ctx.enter_context(tc.tile_pool(name="keep", bufs=1))
+        psum = ctx.enter_context(tc.psum_pool(name="psum", bufs=1))
+
+        list_a = keep.tile([P, J // 16], U16, name="list_a")
+        list_b = keep.tile([P, J // 16], U16, name="list_b")
+        xt_plane = keep.tile([P, PASSES * T], U8, name="xt_plane", align_bytes=64)
+        wa_plane = keep.tile([P, PASSES * N], U8, name="wa_plane", align_bytes=64)
+        xt_tab = [keep.tile([P, T], I32, name="xt_tab%d" % z, align_bytes=64) for z in range(PASSES)]
+        wa_tab = keep.tile([P, PASSES * N], I32, name="wa_tab", align_bytes=64)
+        wb_raw = [keep.tile([P, PACK, N], F32, name="wb_raw%d" % z, align_bytes=64) for z in range(PASSES)]
+        bias_col = keep.tile([P, 2], F32, name="bias_col")
+
+        nc.gpsimd.memset(xt_plane[:].bitcast(I32), 0)
+        nc.vector.memset(wa_plane[:].bitcast(I32), 0)
+
+        def load_plane(plane, scales):
+            rows = scales.bitcast(I32).rearrange("z (q r) c -> r q z c", r=4)
+            dest = plane[:].bitcast(I32).rearrange("p (z c) -> p z c", z=PASSES)
+            for r in range(4):
+                nc.sync.dma_start(out=dest[r:P:32], in_=rows[r])
+
+        nc.sync.dma_start(list_b[:], offs2)
+        nc.sync.dma_start(list_a[:], offs)
+        load_plane(xt_plane, xt_scales)
+        for z in range(PASSES):
+            rows = wb[z * P * PACK : (z + 1) * P * PACK, :]
+            nc.sync.dma_start(out=wb_raw[z][:], in_=rows.rearrange("(p j) n -> p j n", j=PACK))
+        nc.sync.dma_start(out=bias_col[:], in_=bi.rearrange("o (p e) -> (o p) e", e=2))
+        xt_view = xt_words.rearrange("z p c r -> z p (c r)").bitcast(I32)
+        nc.sync.dma_start(out=xt_tab[0][:], in_=xt_view[0])
+        load_plane(wa_plane, wa_scales)
+        nc.sync.dma_start(out=xt_tab[1][:], in_=xt_view[1])
+        nc.sync.dma_start(
+            out=wa_tab[:].rearrange("p (z c) -> p z c", z=PASSES),
+            in_=wa_words.rearrange("z p c r -> p z (c r)").bitcast(I32),
+        )
+
+        def gather_scales(name, offsets):
+            planes = []
+            for z in range(PASSES):
+                picked = keep.tile([P, J], U8, name="%s_plane%d" % (name, z), align_bytes=64)
+                nc.vector.tensor_copy(picked[:], xt_plane[:, z * T : (z + 1) * T].indirect(offsets[:]))
+                planes.append(picked)
+            return planes
+
+        def gather_words(name, offsets, z):
+            picked = keep.tile([P, J], U32, name="%s_words%d" % (name, z), align_bytes=64)
+            nc.vector.tensor_copy(picked[:], xt_tab[z][:].bitcast(U32).indirect(offsets[:]))
+            return picked
+
+        xb_plane = gather_scales("xb", list_b)
+        xa_plane = gather_scales("xa", list_a)
+
+        wb_words, wb_plane = [], []
+        for z in range(PASSES):
+            grouped = keep.tile([P, N * PACK], BF16, name="grouped%d" % z, align_bytes=64)
+            nc.scalar.activation(
+                out=grouped[:].rearrange("p (c i t) -> p c t i", i=4, t=PACK),
+                in_=wb_raw[z][:].rearrange("p t (c i) -> p c t i", i=4),
+                func=COPY,
+            )
+            words = keep.tile([P, N], U32, name="wb_words%d" % z, align_bytes=64)
+            plane = keep.tile([P, N], U8, name="wb_plane%d" % z, align_bytes=64)
+            nc.vector.quantize_mx(out=words[:].bitcast(E4M3), scales=plane[:], in_=grouped[:])
+            wb_words.append(words)
+            wb_plane.append(plane)
+
+        ident = keep.tile([P, P], F32, name="ident")
+        make_identity(nc, ident[:])
+        bias_ps = psum.tile([P, 2, P], F32, name="bias_ps")
+        for e in range(2):
+            nc.tensor.transpose(bias_ps[:, e, :], bias_col[:, e : e + 1].to_broadcast([P, P]), ident[:])
+        bias_rows = keep.tile([P, N], F32, name="bias_rows")
+        nc.scalar.activation(
+            out=bias_rows[:].rearrange("p (c e) -> p c e", e=2),
+            in_=bias_ps[:].rearrange("p e c -> p c e"),
+            func=COPY,
+            scale=GAIN,
+        )
+
+        xb_words, xa_words = [], []
+        for z in range(PASSES):
+            xb_words.append(gather_words("xb", list_b, z))
+            xa_words.append(gather_words("xa", list_a, z))
+
+        def product(name, t, x_words, x_plane, moving):
+            acc = psum.tile([P, N], F32, name="%s%d" % (name, t))
+            cols = slice(t * P, (t + 1) * P)
+            for z in range(PASSES):
+                w_words, w_plane = moving(z)
+                nc.tensor.matmul_mx(
+                    out=acc[:],
+                    lhsT=x_words[z][:, cols].bitcast(E5M2),
+                    lhsT_scale=x_plane[z][:, cols],
+                    rhs=w_words,
+                    rhs_scale=w_plane,
+                    start=(z == 0),
+                    stop=(z == PASSES - 1),
+                )
+            return acc
+
+        def wb_pass(z):
+            return wb_words[z][:].bitcast(E4M3), wb_plane[z][:]
+
+        def wa_pass(z):
+            cols = slice(z * N, (z + 1) * N)
+            return wa_tab[:, cols].bitcast(E5M2), wa_plane[:, cols]
+
+        acc_b = [product("acc_b", t, xb_words, xb_plane, wb_pass) for t in range(TILES)]
+        acc_a = [product("acc_a", t, xa_words, xa_plane, wa_pass) for t in range(TILES)]
+
+        neg_b, peak_b = [], []
+        for t in range(TILES):
+            rows = keep.tile([P, N], F32, name="neg_b%d" % t)
+            nc.vector.scalar_tensor_tensor(
+                out=rows[:], in0=acc_b[t][:], scalar=-GAIN, in1=bias_rows[:], op0=ALU.mult, op1=ALU.subtract
+            )
+            neg_b.append(rows)
+        for t in range(TILES):
+            peak = keep.tile([P, 1], F32, name="peak_b%d" % t)
+            nc.vector.tensor_reduce(out=peak[:], in_=neg_b[t][:], axis=AXIS_X, op=ALU.max, apply_absolute_value=True)
+            peak_b.append(peak)
+
+        peak_a, first = [], []
+        for t in range(TILES):
+            a_rows = keep.tile([P, N], F32, name="a_rows%d" % t)
+            nc.scalar.activation(out=a_rows[:], in_=acc_a[t][:], func=COPY)
+            peak = keep.tile([P, 1], F32, name="peak_a%d" % t)
+            nc.vector.tensor_reduce(out=peak[:], in_=a_rows[:], axis=AXIS_X, op=ALU.max, apply_absolute_value=True)
+            peak_a.append(peak)
+        for t in range(TILES):
+            term = keep.tile([P, N], F32, name="first%d" % t)
+            nc.scalar.activation(out=term[:], in_=acc_a[t][:], func=COPY, scale=peak_b[t][:])
+            first.append(term)
+        for t in range(TILES):
+            result = keep.tile([P, N], F32, name="result%d" % t)
+            nc.vector.scalar_tensor_tensor(
+                out=result[:], in0=neg_b[t][:], scalar=peak_a[t][:], in1=first[t][:], op0=ALU.mult, op1=ALU.add
+            )
+            (nc.sync, nc.scalar)[t].dma_start(out=out[t * P : (t + 1) * P, :], in_=result[:])

@@ -23,6 +23,7 @@ PACK = 4
 PASSES = K // (P * PACK)
 TILES = J // P
 GAIN = 0.3
+VECTOR_COLS = (256, 256)
 
 
 def tile_list_rows_twotokens_crosspeaks_kernel(tc, xt_words, xt_scales, wa_words, wa_scales, wb, bi, offs, offs2, out):
@@ -33,7 +34,7 @@ def tile_list_rows_twotokens_crosspeaks_kernel(tc, xt_words, xt_scales, wa_words
 
         list_a = keep.tile([P, J // 16], U16, name="list_a")
         list_b = keep.tile([P, J // 16], U16, name="list_b")
-        xt_plane = keep.tile([P, PASSES * T], U8, name="xt_plane", align_bytes=64)
+        xt_plane = keep.tile([P, T], U8, name="xt_plane", align_bytes=64)
         wa_plane = keep.tile([P, PASSES * N], U8, name="wa_plane", align_bytes=64)
         xt_tab = [keep.tile([P, T], I32, name="xt_tab%d" % z, align_bytes=64) for z in range(PASSES)]
         wa_tab = keep.tile([P, PASSES * N], I32, name="wa_tab", align_bytes=64)
@@ -43,52 +44,60 @@ def tile_list_rows_twotokens_crosspeaks_kernel(tc, xt_words, xt_scales, wa_words
         nc.gpsimd.memset(xt_plane[:].bitcast(I32), 0)
         nc.vector.memset(wa_plane[:].bitcast(I32), 0)
 
-        def load_plane(plane, scales):
+        def load_plane(queues, plane, scales):
             rows = scales.bitcast(I32).rearrange("z (q r) c -> r q z c", r=4)
             dest = plane[:].bitcast(I32).rearrange("p (z c) -> p z c", z=PASSES)
             for r in range(4):
-                nc.sync.dma_start(out=dest[r:P:32], in_=rows[r])
+                queues[r].dma_start(out=dest[r:P:32], in_=rows[r])
 
-        nc.sync.dma_start(list_b[:], offs2)
-        nc.sync.dma_start(list_a[:], offs)
-        load_plane(xt_plane, xt_scales)
-        for z in range(PASSES):
+        def load_wb(z):
             rows = wb[z * P * PACK : (z + 1) * P * PACK, :]
             nc.sync.dma_start(out=wb_raw[z][:], in_=rows.rearrange("(p j) n -> p j n", j=PACK))
-        nc.sync.dma_start(out=bias_col[:], in_=bi.rearrange("o (p e) -> (o p) e", e=2))
+
+        def load_xt_plane(queues):
+            rows = xt_scales.bitcast(I32)
+            dest = xt_plane[:].bitcast(I32)
+            for q in range(4):
+                queues[q].dma_start(out=dest[32 * q : 32 * q + 8, :], in_=rows[:, 4 * q : 4 * q + 4, :])
+
         xt_view = xt_words.rearrange("z p c r -> z p (c r)").bitcast(I32)
+        nc.sync.dma_start(list_b[:], offs2)
+        load_xt_plane((nc.sync, nc.scalar, nc.sync, nc.scalar))
+        nc.scalar.dma_start(out=bias_col[:], in_=bi.rearrange("o (p e) -> (o p) e", e=2))
+        nc.sync.dma_start(list_a[:], offs)
+        load_wb(0)
+        load_wb(1)
         nc.sync.dma_start(out=xt_tab[0][:], in_=xt_view[0])
-        load_plane(wa_plane, wa_scales)
         nc.sync.dma_start(out=xt_tab[1][:], in_=xt_view[1])
         nc.sync.dma_start(
             out=wa_tab[:].rearrange("p (z c) -> p z c", z=PASSES),
             in_=wa_words.rearrange("z p c r -> p z (c r)").bitcast(I32),
         )
+        load_plane((nc.sync,) * 4, wa_plane, wa_scales)
 
-        def gather_scales(name, offsets):
-            planes = []
-            for z in range(PASSES):
-                picked = keep.tile([P, J], U8, name="%s_plane%d" % (name, z), align_bytes=64)
-                nc.vector.tensor_copy(picked[:], xt_plane[:, z * T : (z + 1) * T].indirect(offsets[:]))
-                planes.append(picked)
-            return planes
+        picked = keep.tile([P, 2 * J], U8, name="picked", align_bytes=64)
+        moved = keep.tile([P, 2 * J], U8, name="moved", align_bytes=64)
+        nc.gpsimd.memset(moved[:].bitcast(I32), 0)
+        nc.vector.tensor_copy(picked[:, 0:J], xt_plane[:].indirect(list_b[:]))
+        nc.vector.tensor_copy(picked[:, J : 2 * J], xt_plane[:].indirect(list_a[:]))
+        nc.scalar.dma_start(out=moved[0:112, :].bitcast(I32), in_=picked[4:116, :].bitcast(I32))
+        xb_plane = [picked[:, 0:J], moved[:, 0:J]]
+        xa_plane = [picked[:, J : 2 * J], moved[:, J : 2 * J]]
 
         def gather_words(name, offsets, z):
             picked = keep.tile([P, J], U32, name="%s_words%d" % (name, z), align_bytes=64)
             nc.vector.tensor_copy(picked[:], xt_tab[z][:].bitcast(U32).indirect(offsets[:]))
             return picked
 
-        xb_plane = gather_scales("xb", list_b)
-        xa_plane = gather_scales("xa", list_a)
-
         wb_words, wb_plane = [], []
         for z in range(PASSES):
             grouped = keep.tile([P, N * PACK], BF16, name="grouped%d" % z, align_bytes=64)
-            nc.scalar.activation(
-                out=grouped[:].rearrange("p (c i t) -> p c t i", i=4, t=PACK),
-                in_=wb_raw[z][:].rearrange("p t (c i) -> p c t i", i=4),
-                func=COPY,
-            )
+            dest = grouped[:].rearrange("p (c i t) -> p c t i", i=4, t=PACK)
+            source = wb_raw[z][:].rearrange("p t (c i) -> p c t i", i=4)
+            cut = VECTOR_COLS[z] // 4
+            nc.vector.tensor_copy(out=dest[:, 0:cut], in_=source[:, 0:cut])
+            if cut < N // 4:
+                nc.scalar.activation(out=dest[:, cut:], in_=source[:, cut:], func=COPY)
             words = keep.tile([P, N], U32, name="wb_words%d" % z, align_bytes=64)
             plane = keep.tile([P, N], U8, name="wb_plane%d" % z, align_bytes=64)
             nc.vector.quantize_mx(out=words[:].bitcast(E4M3), scales=plane[:], in_=grouped[:])
@@ -97,16 +106,13 @@ def tile_list_rows_twotokens_crosspeaks_kernel(tc, xt_words, xt_scales, wa_words
 
         ident = keep.tile([P, P], F32, name="ident")
         make_identity(nc, ident[:])
-        bias_ps = psum.tile([P, 2, P], F32, name="bias_ps")
-        for e in range(2):
-            nc.tensor.transpose(bias_ps[:, e, :], bias_col[:, e : e + 1].to_broadcast([P, P]), ident[:])
+        bias_gain = keep.tile([P, 2], F32, name="bias_gain")
+        nc.scalar.activation(out=bias_gain[:], in_=bias_col[:], func=COPY, scale=GAIN)
         bias_rows = keep.tile([P, N], F32, name="bias_rows")
-        nc.scalar.activation(
-            out=bias_rows[:].rearrange("p (c e) -> p c e", e=2),
-            in_=bias_ps[:].rearrange("p e c -> p c e"),
-            func=COPY,
-            scale=GAIN,
-        )
+        for e in range(2):
+            bias_ps = psum.tile([P, P], F32, name="bias_ps%d" % e, tag="acc_b%d" % e)
+            nc.tensor.transpose(bias_ps[:], bias_gain[:, e : e + 1].to_broadcast([P, P]), ident[:])
+            nc.scalar.activation(out=bias_rows[:, e:N:2], in_=bias_ps[:], func=COPY)
 
         xb_words, xa_words = [], []
         for z in range(PASSES):
@@ -114,7 +120,7 @@ def tile_list_rows_twotokens_crosspeaks_kernel(tc, xt_words, xt_scales, wa_words
             xa_words.append(gather_words("xa", list_a, z))
 
         def product(name, t, x_words, x_plane, moving):
-            acc = psum.tile([P, N], F32, name="%s%d" % (name, t))
+            acc = psum.tile([P, N], F32, name="%s%d" % (name, t), tag="%s%d" % (name, t))
             cols = slice(t * P, (t + 1) * P)
             for z in range(PASSES):
                 w_words, w_plane = moving(z)

@@ -23,7 +23,7 @@ PACK = 4
 PASSES = K // (P * PACK)
 TILES = J // P
 GAIN = 0.3
-VECTOR_COLS = (256, 256)
+VECTOR_COLS = (0, 160)
 
 
 def tile_list_rows_twotokens_crosspeaks_kernel(tc, xt_words, xt_scales, wa_words, wa_scales, wb, bi, offs, offs2, out):
@@ -63,10 +63,10 @@ def tile_list_rows_twotokens_crosspeaks_kernel(tc, xt_words, xt_scales, wa_words
         xt_view = xt_words.rearrange("z p c r -> z p (c r)").bitcast(I32)
         nc.sync.dma_start(list_b[:], offs2)
         load_xt_plane((nc.sync, nc.scalar, nc.sync, nc.scalar))
-        nc.scalar.dma_start(out=bias_col[:], in_=bi.rearrange("o (p e) -> (o p) e", e=2))
         nc.sync.dma_start(list_a[:], offs)
         load_wb(0)
         load_wb(1)
+        nc.sync.dma_start(out=bias_col[:], in_=bi.rearrange("o (p e) -> (o p) e", e=2))
         nc.sync.dma_start(out=xt_tab[0][:], in_=xt_view[0])
         nc.sync.dma_start(out=xt_tab[1][:], in_=xt_view[1])
         nc.sync.dma_start(
@@ -80,7 +80,7 @@ def tile_list_rows_twotokens_crosspeaks_kernel(tc, xt_words, xt_scales, wa_words
         nc.gpsimd.memset(moved[:].bitcast(I32), 0)
         nc.vector.tensor_copy(picked[:, 0:J], xt_plane[:].indirect(list_b[:]))
         nc.vector.tensor_copy(picked[:, J : 2 * J], xt_plane[:].indirect(list_a[:]))
-        nc.scalar.dma_start(out=moved[0:112, :].bitcast(I32), in_=picked[4:116, :].bitcast(I32))
+        nc.gpsimd.dma_start(out=moved[0:112, :].bitcast(I32), in_=picked[4:116, :].bitcast(I32))
         xb_plane = [picked[:, 0:J], moved[:, 0:J]]
         xa_plane = [picked[:, J : 2 * J], moved[:, J : 2 * J]]
 
@@ -95,9 +95,9 @@ def tile_list_rows_twotokens_crosspeaks_kernel(tc, xt_words, xt_scales, wa_words
             dest = grouped[:].rearrange("p (c i t) -> p c t i", i=4, t=PACK)
             source = wb_raw[z][:].rearrange("p t (c i) -> p c t i", i=4)
             cut = VECTOR_COLS[z] // 4
-            nc.vector.tensor_copy(out=dest[:, 0:cut], in_=source[:, 0:cut])
-            if cut < N // 4:
-                nc.scalar.activation(out=dest[:, cut:], in_=source[:, cut:], func=COPY)
+            if cut:
+                nc.vector.tensor_copy(out=dest[:, 0:cut], in_=source[:, 0:cut])
+            nc.scalar.activation(out=dest[:, cut:], in_=source[:, cut:], func=COPY)
             words = keep.tile([P, N], U32, name="wb_words%d" % z, align_bytes=64)
             plane = keep.tile([P, N], U8, name="wb_plane%d" % z, align_bytes=64)
             nc.vector.quantize_mx(out=words[:].bitcast(E4M3), scales=plane[:], in_=grouped[:])
@@ -106,13 +106,11 @@ def tile_list_rows_twotokens_crosspeaks_kernel(tc, xt_words, xt_scales, wa_words
 
         ident = keep.tile([P, P], F32, name="ident")
         make_identity(nc, ident[:])
-        bias_gain = keep.tile([P, 2], F32, name="bias_gain")
-        nc.scalar.activation(out=bias_gain[:], in_=bias_col[:], func=COPY, scale=GAIN)
         bias_rows = keep.tile([P, N], F32, name="bias_rows")
         for e in range(2):
             bias_ps = psum.tile([P, P], F32, name="bias_ps%d" % e, tag="acc_b%d" % e)
-            nc.tensor.transpose(bias_ps[:], bias_gain[:, e : e + 1].to_broadcast([P, P]), ident[:])
-            nc.scalar.activation(out=bias_rows[:, e:N:2], in_=bias_ps[:], func=COPY)
+            nc.tensor.transpose(bias_ps[:], bias_col[:, e : e + 1].to_broadcast([P, P]), ident[:])
+            nc.scalar.activation(out=bias_rows[:, e:N:2], in_=bias_ps[:], func=COPY, scale=GAIN)
 
         xb_words, xa_words = [], []
         for z in range(PASSES):

from contextlib import ExitStack

import concourse.mybir as mybir
from concourse.masks import make_identity

K, T, J, N = 1024, 1024, 256, 256
FLOPS = 2 * 2 * J * K * N

F32 = mybir.dt.float32
BF16 = mybir.dt.bfloat16
I32 = mybir.dt.int32
U32 = mybir.dt.uint32
U16 = mybir.dt.uint16
U8 = mybir.dt.uint8
E4M3 = mybir.dt.float8_e4m3fn_x4
E5M2 = mybir.dt.float8_e5m2_x4
ALU = mybir.AluOpType
COPY = mybir.ActivationFunctionType.Copy
AXIS_X = mybir.AxisListType.X

P = 128
PACK = 4
PASSES = K // (P * PACK)
TILES = J // P
GAIN = 0.3
VECTOR_COLS = (0, 160)


def tile_list_rows_twotokens_crosspeaks_kernel(tc, xt_words, xt_scales, wa_words, wa_scales, wb, bi, offs, offs2, out):
    nc = tc.nc
    with ExitStack() as ctx:
        keep = ctx.enter_context(tc.tile_pool(name="keep", bufs=1))
        psum = ctx.enter_context(tc.psum_pool(name="psum", bufs=1))

        list_a = keep.tile([P, J // 16], U16, name="list_a")
        list_b = keep.tile([P, J // 16], U16, name="list_b")
        xt_plane = keep.tile([P, T], U8, name="xt_plane", align_bytes=64)
        wa_plane = keep.tile([P, PASSES * N], U8, name="wa_plane", align_bytes=64)
        xt_tab = [keep.tile([P, T], I32, name="xt_tab%d" % z, align_bytes=64) for z in range(PASSES)]
        wa_tab = keep.tile([P, PASSES * N], I32, name="wa_tab", align_bytes=64)
        wb_raw = [keep.tile([P, PACK, N], F32, name="wb_raw%d" % z, align_bytes=64) for z in range(PASSES)]
        bias_col = keep.tile([P, 2], F32, name="bias_col")

        nc.gpsimd.memset(xt_plane[:].bitcast(I32), 0)
        nc.vector.memset(wa_plane[:].bitcast(I32), 0)

        def load_plane(queues, plane, scales):
            rows = scales.bitcast(I32).rearrange("z (q r) c -> r q z c", r=4)
            dest = plane[:].bitcast(I32).rearrange("p (z c) -> p z c", z=PASSES)
            for r in range(4):
                queues[r].dma_start(out=dest[r:P:32], in_=rows[r])

        def load_wb(z):
            rows = wb[z * P * PACK : (z + 1) * P * PACK, :]
            nc.sync.dma_start(out=wb_raw[z][:], in_=rows.rearrange("(p j) n -> p j n", j=PACK))

        def load_xt_plane(queues):
            rows = xt_scales.bitcast(I32)
            dest = xt_plane[:].bitcast(I32)
            for q in range(4):
                queues[q].dma_start(out=dest[32 * q : 32 * q + 8, :], in_=rows[:, 4 * q : 4 * q + 4, :])

        xt_view = xt_words.rearrange("z p c r -> z p (c r)").bitcast(I32)
        nc.sync.dma_start(list_b[:], offs2)
        load_xt_plane((nc.sync, nc.scalar, nc.sync, nc.scalar))
        nc.sync.dma_start(list_a[:], offs)
        load_wb(0)
        load_wb(1)
        nc.sync.dma_start(out=bias_col[:], in_=bi.rearrange("o (p e) -> (o p) e", e=2))
        nc.sync.dma_start(out=xt_tab[0][:], in_=xt_view[0])
        nc.sync.dma_start(out=xt_tab[1][:], in_=xt_view[1])
        nc.sync.dma_start(
            out=wa_tab[:].rearrange("p (z c) -> p z c", z=PASSES),
            in_=wa_words.rearrange("z p c r -> p z (c r)").bitcast(I32),
        )
        load_plane((nc.sync,) * 4, wa_plane, wa_scales)

        picked = keep.tile([P, 2 * J], U8, name="picked", align_bytes=64)
        moved = keep.tile([P, 2 * J], U8, name="moved", align_bytes=64)
        nc.gpsimd.memset(moved[:].bitcast(I32), 0)
        nc.vector.tensor_copy(picked[:, 0:J], xt_plane[:].indirect(list_b[:]))
        nc.vector.tensor_copy(picked[:, J : 2 * J], xt_plane[:].indirect(list_a[:]))
        nc.gpsimd.dma_start(out=moved[0:112, :].bitcast(I32), in_=picked[4:116, :].bitcast(I32))
        xb_plane = [picked[:, 0:J], moved[:, 0:J]]
        xa_plane = [picked[:, J : 2 * J], moved[:, J : 2 * J]]

        def gather_words(name, offsets, z):
            picked = keep.tile([P, J], U32, name="%s_words%d" % (name, z), align_bytes=64)
            nc.vector.tensor_copy(picked[:], xt_tab[z][:].bitcast(U32).indirect(offsets[:]))
            return picked

        wb_words, wb_plane = [], []
        for z in range(PASSES):
            grouped = keep.tile([P, N * PACK], BF16, name="grouped%d" % z, align_bytes=64)
            dest = grouped[:].rearrange("p (c i t) -> p c t i", i=4, t=PACK)
            source = wb_raw[z][:].rearrange("p t (c i) -> p c t i", i=4)
            cut = VECTOR_COLS[z] // 4
            if cut:
                nc.vector.tensor_copy(out=dest[:, 0:cut], in_=source[:, 0:cut])
            nc.scalar.activation(out=dest[:, cut:], in_=source[:, cut:], func=COPY)
            words = keep.tile([P, N], U32, name="wb_words%d" % z, align_bytes=64)
            plane = keep.tile([P, N], U8, name="wb_plane%d" % z, align_bytes=64)
            nc.vector.quantize_mx(out=words[:].bitcast(E4M3), scales=plane[:], in_=grouped[:])
            wb_words.append(words)
            wb_plane.append(plane)

        ident = keep.tile([P, P], F32, name="ident")
        make_identity(nc, ident[:])
        bias_rows = keep.tile([P, N], F32, name="bias_rows")
        for e in range(2):
            bias_ps = psum.tile([P, P], F32, name="bias_ps%d" % e, tag="acc_b%d" % e)
            nc.tensor.transpose(bias_ps[:], bias_col[:, e : e + 1].to_broadcast([P, P]), ident[:])
            nc.scalar.activation(out=bias_rows[:, e:N:2], in_=bias_ps[:], func=COPY, scale=GAIN)

        xb_words, xa_words = [], []
        for z in range(PASSES):
            xb_words.append(gather_words("xb", list_b, z))
            xa_words.append(gather_words("xa", list_a, z))

        def product(name, t, x_words, x_plane, moving):
            acc = psum.tile([P, N], F32, name="%s%d" % (name, t), tag="%s%d" % (name, t))
            cols = slice(t * P, (t + 1) * P)
            for z in range(PASSES):
                w_words, w_plane = moving(z)
                nc.tensor.matmul_mx(
                    out=acc[:],
                    lhsT=x_words[z][:, cols].bitcast(E5M2),
                    lhsT_scale=x_plane[z][:, cols],
                    rhs=w_words,
                    rhs_scale=w_plane,
                    start=(z == 0),
                    stop=(z == PASSES - 1),
                )
            return acc

        def wb_pass(z):
            return wb_words[z][:].bitcast(E4M3), wb_plane[z][:]

        def wa_pass(z):
            cols = slice(z * N, (z + 1) * N)
            return wa_tab[:, cols].bitcast(E5M2), wa_plane[:, cols]

        acc_b = [product("acc_b", t, xb_words, xb_plane, wb_pass) for t in range(TILES)]
        acc_a = [product("acc_a", t, xa_words, xa_plane, wa_pass) for t in range(TILES)]

        neg_b, peak_b = [], []
        for t in range(TILES):
            rows = keep.tile([P, N], F32, name="neg_b%d" % t)
            nc.vector.scalar_tensor_tensor(
                out=rows[:], in0=acc_b[t][:], scalar=-GAIN, in1=bias_rows[:], op0=ALU.mult, op1=ALU.subtract
            )
            neg_b.append(rows)
        for t in range(TILES):
            peak = keep.tile([P, 1], F32, name="peak_b%d" % t)
            nc.vector.tensor_reduce(out=peak[:], in_=neg_b[t][:], axis=AXIS_X, op=ALU.max, apply_absolute_value=True)
            peak_b.append(peak)

        peak_a, first = [], []
        for t in range(TILES):
            a_rows = keep.tile([P, N], F32, name="a_rows%d" % t)
            nc.scalar.activation(out=a_rows[:], in_=acc_a[t][:], func=COPY)
            peak = keep.tile([P, 1], F32, name="peak_a%d" % t)
            nc.vector.tensor_reduce(out=peak[:], in_=a_rows[:], axis=AXIS_X, op=ALU.max, apply_absolute_value=True)
            peak_a.append(peak)
        for t in range(TILES):
            term = keep.tile([P, N], F32, name="first%d" % t)
            nc.scalar.activation(out=term[:], in_=acc_a[t][:], func=COPY, scale=peak_b[t][:])
            first.append(term)
        for t in range(TILES):
            result = keep.tile([P, N], F32, name="result%d" % t)
            nc.vector.scalar_tensor_tensor(
                out=result[:], in0=neg_b[t][:], scalar=peak_a[t][:], in1=first[t][:], op0=ALU.mult, op1=ALU.add
            )
            (nc.sync, nc.scalar)[t].dma_start(out=out[t * P : (t + 1) * P, :], in_=result[:])
